import numpy as np, ml_dtypes
CORES = [1,5,17,21,33,37,49,53]
N = 8
BF = ml_dtypes.bfloat16
def gentries(a):
    return np.ascontiguousarray(a.reshape(8, 16, -1).transpose(0, 2, 1)).reshape(8, -1)
def gtable(e):
    e = np.asarray(e); return np.ascontiguousarray(e.reshape(8, -1, 16).transpose(0, 2, 1)).reshape(128, -1).astype(np.int32)
V, K, C, M, T, H, LX = 4096, 4096, 8, 4, 5, 3, 63
TH = np.array([60, 64, 68])
LA = K // C
def parts(rng):
    w = np.floor(256 * rng.random((N, 8, 16, V)) * rng.random((N, 8, 16, V)))
    l = 1 + np.floor(LX * rng.random((N, 8, V)) * rng.random((N, 8, V))).astype(np.int64)
    d = np.argsort(rng.random((N, 8, M, V)), axis=-1)
    o = np.floor(LX * rng.random((N, 8, M, V)) * rng.random((N, 8, M, V))).astype(np.int64)
    b = rng.integers(0, V, (N, 8, LA, C)); c = np.floor(LX * rng.random((N, 8, LA, C)) * rng.random((N, 8, LA, C))).astype(np.int64)
    return w, l, d, o, b, c
def pack(w, l, d, o, b, c):
    return {"wp": np.ascontiguousarray(w.reshape(N, 128, V)).astype(np.float32).astype(BF), "rl": np.ascontiguousarray(l).astype(np.int32),
            "dm": np.ascontiguousarray(d.reshape(N, 8, M * V)).astype(np.int32), "om": np.ascontiguousarray(o.reshape(N, 8, M * V)).astype(np.int32),
            "cb": np.stack([gtable(a.reshape(8, -1)) for a in b]), "co": np.stack([gtable(a.reshape(8, -1)) for a in c])}
def setup_inputs(rng):
    return pack(*parts(rng))
def setup_inputs_spread(rng):
    bits = LX.bit_length()
    w = np.floor(np.exp2(8 * rng.random((N, 8, 1, V))) * rng.random((N, 8, 16, V)) * (rng.random((N, 8, 1, V)) > 0.0625))
    l = np.floor(np.exp2(bits * rng.random((N, 8, V)))).astype(np.int64)
    d = np.floor(V * rng.random((N, 8, M, V)) ** 3).astype(np.int64)
    o = np.floor(np.exp2(bits * rng.random((N, 8, M, V)))).astype(np.int64) - 1
    b = V - 1 - np.floor(V * rng.random((N, 8, LA, C)) ** 3).astype(np.int64)
    c = np.floor(np.exp2(bits * rng.random((N, 8, LA, C)))).astype(np.int64) - 1
    return pack(w, np.clip(l, 1, LX), np.clip(d, 0, V - 1), np.clip(o, 0, LX - 1), np.clip(b, 0, V - 1), np.clip(c, 0, LX - 1))
def setup_inputs_ends(rng):
    def ends(lo, hi, *shape): return np.where(rng.random(shape) < 0.5, lo, hi)
    s0 = V // 4; n0 = V * 3 // 8; mid = slice(s0, s0 + n0)
    share = np.broadcast_to(np.where(rng.random((N, 1, 1, V)) < 0.5, 0.9, 0.1), (N, 8, 16, V)).copy(); share[:, :, [3, 8, 15]] = 0.005
    w = np.where(rng.random((N, 8, 16, V)) < share, 255, 0); w[..., 0] = 0; w[..., V - 1] = 0
    full = [V - 1 if q % 2 == 1 or q == N - 1 else 0 for q in range(N)]
    for q in range(N): w[q, :, :, full[q]] = 255
    l = ends(1, LX, N, 8, V); l[..., mid] = ends(1, LX, N, 1, n0)
    d = ends(0, V - 1, N, 8, M, V); d[..., mid] = s0 + rng.integers(0, n0 - H, (N, 1, M, n0))
    o = ends(0, LX - 1, N, 8, M, V); o[..., mid] = ends(0, LX - 1, N, 1, M, n0)
    b = ends(0, V - 1, N, 8, LA, C); c = ends(0, LX - 1, N, 8, LA, C)
    quiet = rng.permutation(np.arange(3, LA - 2))[:LA * 3 // 8]; nq = len(quiet)
    b[:, :, quiet] = s0 + rng.integers(0, n0 - H, (N, 1, nq, C)); c[:, :, quiet] = ends(0, LX - 1, N, 1, nq, C)
    for i in (0, 1, 2, LA - 2, LA - 1):
        for q in range(N): b[q, :, i] = np.where((np.arange(C) + i + (LA - 1) + (C - 1)) % 2 == 0, full[q], V - 1 - full[q])
    return pack(w, l, d, o, b, c)
def setup_inputs_brink(rng):
    w, l, d, o, b, c = parts(rng); n8 = V // 8
    levels = np.array(sorted(set([0, 1, 127, 128] + [int(v) for h in TH for v in (h - 1, h, 128 - h, 129 - h)])))
    lev = np.repeat(rng.choice(levels, (N, n8)), 8, axis=1)[:, None, None, :]
    late = np.zeros((N, 8, 16)); late[0::4, :, 8:] = 1; late[1::4, :, :8] = 1; late[2::4, 4:] = 1
    pos = np.argsort(np.argsort((rng.random((N, 8, 16)) + late).reshape(N, 128), axis=1), axis=1).reshape(N, 8, 16, 1)
    lo = rng.integers(0, 255, (N, 8, 16, 1)); hi = lo + 1 + np.floor((255 - lo) * rng.random((N, 8, 16, 1))).astype(np.int64)
    rich = np.repeat(rng.random((N, n8)) < 0.3, 8, axis=1)[:, None, None, :]
    w = np.where(rich, w, np.where(pos < lev, hi, lo))
    d = 8 * np.repeat(np.argsort(rng.random((N, 1, M, n8)), axis=-1), 8, axis=-1) + rng.integers(0, 8 - H, (N, 8, M, V))
    b = 8 * rng.integers(0, n8, (N, 1, LA, C)) + rng.integers(0, 8 - H, (N, 8, LA, C))
    for g in range(8):
        s = g // 2
        if g % 2 == 0: lv, ov, cv = [max(s, 1), s + 1, s + 2], [0, 0, 1, s], [s, s, s + 1]
        else: lv, ov, cv = [LX - 1, LX], [0, 1, 2, LX - 1], [LX - 3, LX - 2, LX - 1]
        l[:, g] = rng.choice(np.array(lv), (N, V)); o[:, g] = rng.choice(np.array(ov), (N, M, V)); c[:, g] = rng.choice(np.array(cv), (N, LA, C))
    return pack(w, l, d, o, b, c)
def setup_inputs_corners(rng):
    w, l, d, o, b, c = parts(rng); v = np.arange(V)
    for q in range(N):
        for g in range(8):
            kd = (g + q) % 4; kl = (g // 2 + q) % 4; ko = (g + 2 * q) % 3; z = rng.random((M, V)) < 0.25
            if kd == 0: d[q, g, 0] = v; d[q, g, 1:] = v[::-1]
            elif kd == 1: d[q, g] = np.where(z, V - 1 - rng.integers(0, 3, (M, V)), d[q, g])
            elif kd == 2: d[q, g] = np.where(z, (V - 1) * rng.integers(0, 2, (M, V)), d[q, g])
            else: d[q, g] = (v[None, :] + 1 + np.arange(M)[:, None]) % V
            if kl == 0: l[q, g] = 1
            elif kl == 1: l[q, g] = LX
            elif kl == 2: l[q, g] = rng.choice(np.array([1, 2, LX - 1, LX]), V)
            else: l[q, g, V - 3:] = 1; l[q, g, :2] = (1, LX)
            if ko == 0: o[q, g] = 0
            elif ko == 1: o[q, g] = LX - 1
            else: o[q, g] = rng.choice(np.array([0, 1, LX - 2, LX - 1]), (M, V))
    c = np.where(rng.random(c.shape) < 0.5, rng.choice(np.array([0, 1, LX - 2, LX - 1]), c.shape), c)
    b = np.where(rng.random(b.shape) < 0.25, rng.choice(np.array([0, V - 2, V - 1]), b.shape), b)
    b[:, :, 0, 0] = 0; b[:, :, LA - 1, C - 1] = V - 1
    s = 256 // C; p = np.arange(128).reshape(8, 16, 1)
    w[2] = s * (C - 1 - (v - p) % C) + rng.integers(0, s, (8, 16, V))
    for g in range(8):
        bl = np.concatenate([[0], 1 + rng.permutation(LA - 2), [LA - 1]]) % (V // C)
        b[2, g] = C * bl[:, None] + np.arange(C)
    for g in (1, 4, 7):
        w[:, g, rng.integers(0, 16)] = np.where(rng.random((N, V)) * 2 * C < 1, rng.integers(1, 4, (N, V)), 0)
    w[1] = rng.integers(0, 4, (8, 16, 1))
    return pack(w, l, d, o, b, c)
def setup_inputs_crowd(rng):
    w, l, d, o, b, c = parts(rng)
    x = np.argsort(rng.random((N, 8, V)), axis=-1)[..., :3]; wide_x = np.ascontiguousarray(np.broadcast_to(x[:, :, None, :], (N, 8, M, 3)))
    prof = np.zeros((N, 8, 16, 3)); prof[..., 0] = 255; prof[..., 2] = 255
    for q in range(N): prof[q, rng.integers(0, 8), rng.integers(0, 16), 2] = 0
    np.put_along_axis(w, np.ascontiguousarray(np.broadcast_to(x[:, :, None, :], (N, 8, 16, 3))), prof, 3)
    np.put_along_axis(l, x, LX, 2); np.put_along_axis(o, wide_x, rng.integers(0, 4, (N, 8, M, 3)), 3)
    to = np.argsort(rng.random((N, 1, M, 3)), axis=-1); nx = np.broadcast_to(np.roll(x, -1, axis=0)[:, :, None, :], (N, 8, M, 3))
    np.put_along_axis(d, wide_x, np.take_along_axis(nx, np.ascontiguousarray(np.broadcast_to(to, (N, 8, M, 3))), 3), 3)
    one = rng.integers(0, 3, (N, 1, LA, C)); k = np.arange(C)
    one[:, :, LA - 1] = np.where(k % 2 == 1, 0, 1); one[:, :, LA - 2] = np.where(k % 2 == 1, 2, 1)
    one = np.broadcast_to(one, (N, 8, LA, C)).copy(); m = np.zeros((N, 8, LA, C), bool); m[:, :, LA * 3 // 10:] = True
    for q in range(1, N, 2):
        m[q, :3] = True; m[q, 3] = False; one[q, :2] = 0
        one[q, 1, rng.integers(0, LA - 1), rng.integers(0, C)] = 1; one[q, 2] = rng.integers(0, 3, (LA, C))
        m[q, 3, LA - 1] = True; one[q, 2:4, LA - 1] = 0; one[q, 4:, LA - 1] = np.where(k % 2 == 1, 1, 0)
    b = np.where(m, np.take_along_axis(x, one.reshape(N, 8, -1), 2).reshape(N, 8, LA, C), b); c = np.where(m, rng.integers(0, 4, c.shape), c)
    return pack(w, l, d, o, b, c)
def check_inputs(d):
    bad = []
    for k, lo, hi in (("wp", 0, 255), ("rl", 1, LX), ("dm", 0, V - 1), ("om", 0, LX - 1), ("cb", 0, V - 1), ("co", 0, LX - 1)):
        a = np.asarray(d[k]).astype(np.float64)
        if not (np.min(a) >= lo and np.max(a) <= hi): bad.append("range of " + k)
        elif np.any(a != np.floor(a)): bad.append("whole numbers in " + k)
    return bad
def reference(wp, rl, dm, om, cb, co):
    w = wp.astype(np.float32).reshape(N, 8, 16, V); ln = rl.astype(np.int64); dd = dm.astype(np.int64); oo = om.astype(np.int64)
    b = np.stack([gentries(a) for a in cb]).astype(np.int64); o = np.stack([gentries(a) for a in co]).astype(np.int64)
    e = np.zeros((N, 8, 16, LA), np.float32)
    for t in range(T):
        q = (np.arange(N) + t) % N; nx = (q + 1) % N
        x = np.take_along_axis(w[q], b[:, :, None, :], 3).reshape(N, 8, 16, LA, C)
        e = np.maximum(e, np.max(x, axis=4))
        a = np.add.reduce((x > np.roll(x, -1, axis=4)).astype(np.int64).reshape(N, 128, LA, C), axis=1)
        m = np.add.reduce((a[..., None] >= TH).astype(np.int64), axis=3).reshape(N, 1, K)
        ix = m * V + b
        b = np.take_along_axis(dd[q], ix, 2); o = o + np.take_along_axis(oo[q], ix, 2)
        for h in range(H):
            lb = np.take_along_axis(ln[nx], b, 2); hop = o >= lb
            o = np.where(hop, o - lb, o); b = np.where(hop, (b + 1) % V, b)
        o = np.minimum(o, np.take_along_axis(ln[nx], b, 2) - 1)
    return {"yb": np.stack([gtable(a) for a in b]).astype(np.float32), "yo": np.stack([gtable(a) for a in o]).astype(np.float32), "ye": e.reshape(N, 128, LA).astype(BF)}

import math
from concourse.bass import DstId, RemoteDMATransfer
from concourse.mybir import AluOpType as ALU, ActivationFunctionType as AF

V = 4096
VX = 4128
STEPS = 5
NC = 4
PAD = 16

SCRATCH = {
    "wt": ("sbuf", [128, V + 16], "bfloat16"),
    "tab": ("sbuf", [128, 4 * VX], "bfloat16"),
    "lens": ("sbuf", [128, V + 2 * PAD], "bfloat16"),
    "cbi": ("sbuf", [128, 256], "int32"),
    "coi": ("sbuf", [128, 256], "int32"),
    "rli": ("sbuf", [128, 256], "int32"),
    "rlb": ("sbuf", [128, 256], "bfloat16"),
    "rln": ("sbuf", [128, 256], "bfloat16"),
    "dmi": ("sbuf", [128, 8, 128], "int32"),
    "dmf": ("sbuf", [128, 8, 128], "float32"),
    "dml": ("sbuf", [128, 1024], "uint16"),
    "omi": ("sbuf", [128, 1024], "int32"),
    "omb": ("sbuf", [128, 1024], "bfloat16"),
    "vlo": ("sbuf", [128, 256], "bfloat16"),
    "vhi": ("sbuf", [128, 256], "bfloat16"),
    "vhj": ("sbuf", [128, 256], "int32"),
    "vhk": ("sbuf", [128, 256], "int32"),
    "ones": ("sbuf", [128, 128], "bfloat16"),
    "idb": ("sbuf", [128, 128], "bfloat16"),
    "idn": ("sbuf", [128, 128], "bfloat16"),
    "idm": ("sbuf", [128, 128], "bfloat16"),
    "idf": ("sbuf", [128, 128], "float32"),
    "sel": ("sbuf", [128, 128], "bfloat16"),
    "wsrc": ("sbuf", [128, 40], "bfloat16"),
    "wq": ("sbuf", [128, 64], "bfloat16"),
    "band": ("sbuf", [128, 8], "bfloat16"),
    "pick": ("sbuf", [128, 144], "bfloat16"),
    "bias": ("sbuf", [128, 64], "bfloat16"),
    "quart": ("sbuf", [128, 8], "bfloat16"),
    "lanes": ("sbuf", [128, 1024], "bfloat16"),
    "zc": ("sbuf", [128, 520], "bfloat16"),
    "zm": ("sbuf", [128, 16 * NC + 1, 8], "bfloat16"),
    "zo": ("sbuf", [128, 16 * NC + 1, 8], "bfloat16"),
    "zn": ("sbuf", [128, 48 * NC + 1, 8], "bfloat16"),
    "bl": ("sbuf", [128, STEPS * 256], "uint16"),
    "ot": ("sbuf", [128, STEPS * 256], "bfloat16"),
    "sb": ("sbuf", [128, STEPS * 256], "uint16"),
    "so": ("sbuf", [128, STEPS * 256], "bfloat16"),
    "bf": ("sbuf", [128, 256], "float32"),
    "ixl": ("sbuf", [128, 256], "uint16"),
    "x1": ("sbuf", [128, V], "bfloat16"),
    "cm": ("sbuf", [128, V], "bfloat16"),
    "sc": ("sbuf", [128, V], "bfloat16"),
    "x2": ("sbuf", [128, V], "bfloat16"),
    "pb": ("sbuf", [128, NC * 192], "bfloat16"),
    "rb": ("sbuf", [128, NC * 128], "bfloat16"),
    "ec": ("sbuf", [128, STEPS * 512], "bfloat16"),
    "ei": ("sbuf", [128, (STEPS + 1) * 512], "bfloat16"),
    "tmp": ("sbuf", [128, 256], "float32"),
    "fs": ("sbuf", [128, NC * 128], "float32"),
    "fr": ("sbuf", [128, NC * 128], "float32"),
    "pr0": ("psum", [128, 512], "float32"),
    "pr1": ("psum", [128, 512], "float32"),
    "pr2": ("psum", [128, 512], "float32"),
    "pv": ("psum", [128, 512], "float32"),
    "pi": ("psum", [128, 512], "float32"),
    "px0": ("psum", [128, 512], "float32"),
    "px1": ("psum", [128, 512], "float32"),
    "pl": ("psum", [128, 512], "float32"),
}
SEMAPHORES = ["e_pe", "e_dve", "e_act", "e_pool", "sent"] + ["d%d" % i for i in range(40)] + ["a%d" % i for i in range(40)]

GUESS = [dict(cyc=1.04, pec=0.52, gam=1.4, hop=150.0, fix=40.0, dma=2000.0, rem=2200.0, issue=600.0, first=2500.0, load=1.0),
         dict(cyc=0.95, pec=0.45, gam=1.6, hop=200.0, fix=20.0, dma=2300.0, rem=1800.0, issue=400.0, first=3500.0, load=1.5),
         dict(cyc=1.15, pec=0.6, gam=1.2, hop=120.0, fix=60.0, dma=1700.0, rem=3000.0, issue=900.0, first=2000.0, load=0.8)]
SPLIT = ("43",)
PRE_ACT = 9
LATER = {"scan": 2.5, "ec": 2.5, "s_e": 2.5, "R": 1.5, "P": 1.5, "sum": 1.5, "oT": 1.5, "s_o": 1.5}
PLACE = {"G1a": -2.0, "G1b": -1.75, "bfa": -1.9, "rolla": -1.7, "rollb": -1.45, "cmpa": -1.55, "cmpb": -1.3, "votea": -1.1, "clampa": -0.95,
         "ixba": -1.2, "ixa": -0.85, "list2a": -0.75, "scana": -0.5, "eca": -0.2, "s_ea": 0.0, "G2a": -0.5, "G2b": -0.5, "exta": 0.05, "Na": 0.25,
         "backda": 0.2, "bTa": 0.3, "backa": 0.4, "list1a": 0.55, "sa": 0.65, "Ra": 0.35, "Pa": 0.4, "suma": 0.55, "oTa": 0.65, "s_oa": 0.8,
         "moda": 0.55, "fba": 0.6, "backoa": 0.75, "foa": 0.8, "s_arra": 0.0}
FOUND = []
ROUNDS0 = 4000
ROUNDS, SEED, WINDOW, HEAT = 36000, 1, 50.0, 80.0


def build(T, topo, core, P):
    CYC, DMA_LAT, REM_LAT, REM_ISSUE, REM_FIRST, LOAD = P["cyc"], P["dma"], P["rem"], P["issue"], P["first"], P["load"]

    def dve(cyc):
        return P["fix"] + CYC * max(64, cyc)

    def pe(cyc, n=1):
        return 30.0 + P["pec"] * cyc + 5.0 * n

    def gat(n):
        return 65.0 + P["gam"] * n

    n = len(T.cores)
    rank = T.rank_of(core)
    nxt, prv = T.cores[(rank + 1) % n], T.cores[(rank - 1) % n]
    home, guest = T.cores[(rank - (STEPS - 1)) % n], T.cores[(rank + STEPS - 1) % n]
    ops = []
    cnt = {"d": 0, "a": 0}

    def op(eng, fn, r=(), w=(), banks=(), dur=100.0, lat=0.0, kind="c", after=(), name=""):
        o = {"eng": eng, "fn": fn, "r": list(r), "w": list(w), "banks": list(banks), "dur": dur, "lat": lat,
             "kind": kind, "after": list(after), "i": len(ops), "name": name}
        ops.append(o)
        return o

    def dma(eng, pairs, r, w, lat=0.0, name=""):
        sem = "d%d" % cnt["d"]
        cnt["d"] += 1

        def fn(q):
            for out, src in pairs:
                q.dma_start(out, src).then_inc(T.sem[sem], 16)
        o = op(eng, fn, r, w, dur=100.0 * len(pairs), lat=DMA_LAT + lat, kind="dma", name=name)
        o["tok"] = (sem, 16 * len(pairs))
        return o

    def mask_of(engs):
        m = 0
        for e in engs:
            m |= 1 << e
        return m

    def send(dst, src_core, transfers, r, w, lat=0.0, first=False, name=""):
        sem = "a%d" % cnt["a"]
        cnt["a"] += 1
        engs = topo.engines(core, dst)
        part = len(engs) // len(transfers)
        rid, pid, _ = topo.addr(dst)

        def fn(q):
            if len(transfers) == 1 and len(transfers[0][0]) == 1:
                q.remote_dma(transfers[0][1], transfers[0][0][0], T.sem[sem], T.sem.sent, pid, rid, mask_of(engs))
                return
            ts = []
            for k, (srcs, out) in enumerate(transfers):
                m = mask_of(engs[k * part:(k + 1) * part])
                if len(srcs) == 1:
                    ts.append(RemoteDMATransfer(dst_ids=[DstId(rid=rid, pnc=pid)], dma_engine_mask=m, remote_sem=T.sem[sem],
                                                src=srcs[0], dst=out))
                else:
                    ts.append(RemoteDMATransfer(dst_ids=[DstId(rid=rid, pnc=pid)], dma_engine_mask=m, remote_sem=T.sem[sem],
                                                srcs=list(srcs), dsts=[out], alu_op=2))
            q.remote_dma_fused(ts, local_sem=T.sem.sent)
        s = op("pool", fn, r, (), dur=REM_ISSUE + (REM_FIRST if first else lat), kind="rem", name=name)
        s["sent"] = part * len(transfers)
        a = op(None, None, (), w, dur=0.0, lat=REM_LAT, kind="arr", after=[s], name=name + "_arr")
        a["tok"] = (sem, len(topo.engines(src_core, core)) // len(transfers) * len(transfers))
        return a

    def mm(items, r, banks, cyc, name=""):
        def fn(q):
            last = None
            for out, lhs, rhs, st, sp in items:
                last = q.matmul(out, lhs, rhs, st, sp)
            return last
        return op("pe", fn, r, (), banks, pe(cyc, len(items)), name=name)

    def copy(out, src, r, w, cyc, banks=(), name=""):
        return op("dve", lambda q: q.tensor_copy(out, src), r, w, banks, dve(cyc), name=name)

    def ts(out, src, s1, s2, o0, o1, r, w, cyc, banks=(), name=""):
        if o1 is None:
            return op("dve", lambda q: q.tensor_scalar(out, src, s1, None, o0), r, w, banks, dve(cyc), name=name)
        return op("dve", lambda q: q.tensor_scalar(out, src, s1, s2, o0, o1), r, w, banks, dve(cyc), name=name)

    def tt(out, a, b, o, r, w, cyc, banks=(), name=""):
        return op("dve", lambda q: q.tensor_tensor(out, a, b, o), r, w, banks, dve(cyc), name=name)

    def fill(out, val, w, cyc):
        return op("dve", lambda q: q.memset(out, val), (), w, (), dve(cyc), name="fill")

    def select(out, src, pattern, cmp, base, mult, r, w, cols):
        return op("pool", lambda q: q.affine_select(out, src, pattern, cmp, 0.0, base, mult), r, w, (), 170.0 + 2 * CYC * cols, name="select")

    def gather(eng, out, win, off, r, w, num, name=""):
        def fn(q, e):
            if e == "act":
                return q.activation(out, win.indirect(off), AF.Copy)
            return q.tensor_copy(out, win.indirect(off))
        o = op(eng, fn, r, w, (), gat(num), name=name)
        o["kind"] = "g"
        return o

    dma("sp", [(T.rli[:], T.rl[:])], (), ["rli"], name="ld_rl")
    dma("act", [(T.cbi[:], T.cb[:])], (), ["cbi"], name="ld_cb")
    dma("sp", [(T.wt[:, 0:V], T.wp[:]), (T.wt[:, V:V + 16], T.wp[:, 0:16])], (), ["wt"], lat=3000.0 * LOAD, name="ld_wp")
    dma("sp", [(T.dmi[:, gg, :], T.dm[gg:gg + 1, :]) for gg in range(8)], (), ["dmi"], lat=4000.0 * LOAD, name="ld_dm")
    dma("sp", [(T.coi[:], T.co[:])], (), ["coi"], lat=4000.0 * LOAD, name="ld_co")
    dma("sp", [(T.omi[:, 256 * m:256 * m + 256], T.om[:, V * m:V * m + V]) for m in range(4)], (), ["omi"], lat=5000.0 * LOAD, name="ld_om")
    for k, o in enumerate(ops):
        o["bonus"] = 1e6 - 5e4 * k
    fill(T.lens[:], 1.0, ["lens0"], (V + 2 * PAD) // 2)
    copy(T.rlb[:], T.rli[:], ["rli"], ["rlb"], 256, name="rlb")
    send(prv, nxt, [([T.rlb[:]], T.rln[:])], ["rlb"], ["rln"], first=True, name="s_rl")
    fill(T.ones[:], 1.0, ["ones"], 64)
    select(T.idb[:], T.ones[:], [[-1, 128]], ALU.is_equal, 0, 1, ["ones"], ["idb"], 128)
    op("pool", lambda q: q.iota(T.vlo[:], [[1, 256]], 0, 0, allow_small_or_imprecise_dtypes=True), (), ["vlo"], (), 130.0 + 512 * CYC, name="iota")
    op("pool", lambda q: q.iota(T.vhj[:], [[0, 256]], 0, 256), (), ["vhj"], (), 130.0 + 512 * CYC, name="iota")
    ts(T.vhk[:], T.vhj[:], V - 1, None, ALU.bitwise_and, None, ["vhj"], ["vhk"], 256)
    copy(T.vhi[:], T.vhk[:], ["vhk"], ["vhi"], 256)
    copy(T.idf[:], T.idb[:], ["idb"], ["idf"], 128)
    ts(T.idn[:], T.idb[:], -1.0, None, ALU.mult, None, ["idb"], ["idn"], 64)
    ts(T.idm[:], T.idb[:], float(VX), None, ALU.mult, None, ["idb"], ["idm"], 64)
    select(T.sel[:], T.ones[:], [[-8, 2], [-16, 8], [-1, 8]], ALU.is_equal, 0, 1, ["ones"], ["sel"], 128)
    fill(T.wsrc[:], -1.0, ["wsrc0"], 64)
    fill(T.pick[:], 0.0, ["pick"], 72)
    select(T.wsrc[:], T.wsrc[:], [[0, 5], [-16, 8]], ALU.is_ge, 0, 1, ["wsrc0"], ["wsrc0"], 40)
    select(T.wq[:, 40:64], T.ones[:, 0:24], [[-1, 3], [-16, 8]], ALU.is_equal, -1, 1, ["ones"], ["wqb"], 24)
    select(T.band[:], T.ones[:, 0:8], [[-16, 8]], ALU.is_ge, -5, 1, ["ones"], ["band"], 8)
    select(T.wq[:, 0:24], T.wsrc[:, 0:24], [[1, 3], [16, 8]], ALU.is_ge, 1, -1, ["wsrc0"], ["wqa"], 24)
    select(T.wq[:, 24:40], T.wsrc[:, 24:40], [[4, 2], [16, 8]], ALU.is_ge, 0, -1, ["wsrc0"], ["wqc"], 16)
    select(T.pick[:, 15:143:16], T.band[:], [[16, 8]], ALU.is_ge, 6, -1, ["band", "pick"], ["pick"], 8)
    fill(T.bias[0:64, :], 2.0, ["bias0"], 64)
    fill(T.bias[64:96, :], 0.0, ["bias1"], 64)
    fill(T.bias[96:128, :], 5.0 / 256.0, ["bias2"], 64)
    fill(T.quart[:], 0.25, ["quart"], 64)
    fill(T.lanes[:], 1.0, ["lanes"], 512)
    fill(T.lanes[:, 0::8], 0.0, ["lanes"], 64)
    fill(T.zc[:], 0.0, ["zc"], 260)
    fill(T.zm[:, 0::2, :], 0.0, ["zm%d" % c for c in range(NC)], 32 * NC)
    fill(T.zo[:, 0::2, :], 0.0, ["zo%d" % c for c in range(NC)], 32 * NC)
    fill(T.zn[:, 0::2, :], 0.0, ["zn%d" % c for c in range(NC)], 96 * NC)
    dma("sp", [(T.lens[5::16, PAD:PAD + V], T.vlo[:]), (T.lens[6::16, PAD:PAD + V], T.vhi[:])], ["lens0", "vlo", "vhi"], ["lens1"], name="lens_v")
    dma("sp", [(T.lens[1 + s::16, PAD - s:PAD - s + V], T.rln[:]) for s in range(4)]
        + [(T.lens[1 + s::16, PAD - s + V:PAD - s + V + 4], T.rln[0::16, 0:4]) for s in range(1, 4)],
        ["lens0", "rln"], ["lens2"], name="lens_l")
    copy(T.bl[:, 0:256], T.cbi[:], ["cbi"], ["bl0_%d" % c for c in range(NC)], 256, name="bl0")
    copy(T.zc[:, 1:513:2], T.coi[:], ["coi", "zc"], ["zc"], 256, name="zc")
    mm([(T.pl[:, 64 * c:64 * c + 64], T.zc[:, 128 * c + 1 - h:128 * c + 129 - h], T.sel[:, 64 * h:64 * h + 64], h == 0, h == 1)
        for c in range(NC) for h in range(2)], ["zc", "sel"], ["pl"], 512, name="ot0")
    copy(T.ot[:, 0:256], T.pl[:, 0:256], [], ["ot0_%d" % c for c in range(NC)], 256, ["pl"], name="ot0")
    for gg in range(8):
        copy(T.dmf[:, :, 16 * gg:16 * gg + 16], T.dmi[:, gg, :], ["dmi"], ["dmf%d" % gg], 128, name="dmf")
    for h in range(2):
        px = T["px%d" % h]
        mm([(px[:, u::8], T.dmf[:, u, :], T.idf[:, 64 * h:64 * h + 64], True, True) for u in range(8)],
           ["dmf%d" % gg for gg in range(8)] + ["idf"], ["px%d" % h], 2048, name="dmT")
        copy(T.dml[:, 512 * h:512 * h + 512], px[:], [], ["dml%d" % h], 512, ["px%d" % h], name="dml")
    for m in range(4):
        ts(T.omb[:, 256 * m:256 * m + 256], T.omi[:, 256 * m:256 * m + 256], -1.0, None, ALU.mult, None, ["omi"], ["omb%d" % m], 256, name="omb")
        for k in range(4):
            piece = 4 * m + k
            gather("act" if (piece + 1) * PRE_ACT // 16 > piece * PRE_ACT // 16 else "dve", T.tab[:, VX * m + 1024 * k:VX * m + 1024 * k + 1024], T.lens[:, PAD:PAD + V],
                   T.dml[:, 256 * m + 64 * k:256 * m + 64 * k + 64], ["lens1", "lens2", "dml%d" % (m // 2)], ["tab%d_%d" % (m, k)], 1024, name="pre")
        keys = ["tab%d_%d" % (m, k) for k in range(4)]
        dma("sp", [(T.tab[0::16, VX * m:VX * m + V], T.omb[:, 256 * m:256 * m + 256])], ["omb%d" % m], keys, name="off")
        copy(T.tab[:, VX * m + V:VX * m + VX], T.tab[:, VX * m:VX * m + VX - V], keys[:1], ["tabw%d" % m], 64, name="wrap")
    tabkeys = ["tab%d_%d" % (m, k) for m in range(4) for k in range(4)] + ["tabw%d" % m for m in range(4)]
    wkeys = ["wqa", "wqb", "wqc"]

    def turn(out, z, c, ident, st, sp):
        return [(out, z[:, 16 * c + 1:16 * c + 17, :], ident[:, 0::2], st, False), (out, z[:, 16 * c:16 * c + 16, :], ident[:, 1::2], False, sp)]

    roll = [0]
    for t in range(STEPS):
        last = t == STEPS - 1
        for c in range(NC):
            j0, s0 = 1024 * c, 256 * t + 64 * c
            nm = "%d%d" % (t, c)
            kb, ko = "bl%d_%d" % (t, c), "ot%d_%d" % (t, c)
            zpad = slice(16 * c + 1, 16 * c + 16, 2)
            copy(T.bf[:, 64 * c:64 * c + 64], T.bl[:, s0:s0 + 64], [kb], ["bf%d" % c], 64, name="bf" + nm)
            for h in range(2):
                a = j0 + 512 * h
                gather("act", T.x1[:, a:a + 512], T.wt[:], T.bl[:, s0 + 32 * h:s0 + 32 * h + 32], [kb, "wt"], ["x1%d%d" % (c, h)], 512, name="G1" + nm)
                bank = "pr%d" % (roll[0] % 3)
                roll[0] += 1
                mm([(T[bank][:, k::8], T.idb[:], T.x1[:, a + (k + 1) % 8:a + 512:8], True, True) for k in range(8)],
                   ["x1%d%d" % (c, h), "idb"], [bank], 512, name="roll" + nm)
                tt(T.cm[:, a:a + 512], T.x1[:, a:a + 512], T[bank][:], ALU.is_gt, ["x1%d%d" % (c, h)], ["cm%d%d" % (c, h)], 512, [bank], name="cmp" + nm)
            mm([(T.pv[:, 0:64], T.ones[:], T.bias[:], True, False)]
               + [(T.pv[:, k:64:8], T.cm[:, j0 + k:j0 + 1024:8], T.quart[:], False, k == 7) for k in range(8)],
               ["cm%d0" % c, "cm%d1" % c, "ones", "bias0", "bias1", "bias2", "quart"], ["pv"], 576, name="vote" + nm)
            ts(T.zm[:, zpad, :], T.pv[:, 0:64], 143.0, 146.0, ALU.max, ALU.min, [], ["zm%d" % c], 64, ["pv"], name="clamp" + nm)
            mm([(T.pi[:, 0:64], T.idf[:], T.bf[:, 64 * c:64 * c + 64], True, False)], ["bf%d" % c, "idf"], ["pi"], 256, name="ixb" + nm)
            mm(turn(T.pi[:, 0:64], T.zm, c, T.idm, False, True), ["zm%d" % c, "idm"], ["pi"], 128, name="ix" + nm)
            ts(T.ixl[:, 64 * c:64 * c + 64], T.pi[:, 0:64], -143.0 * VX, None, ALU.add, None, [], ["ixl%d" % c], 64, ["pi"], name="list2" + nm)
            op("dve", lambda q, j0=j0: q.tensor_tensor_scan(T.sc[:, j0:j0 + 1024], T.lanes[:], T.x1[:, j0:j0 + 1024], 0.0, ALU.mult, ALU.max),
               ["x1%d0" % c, "x1%d1" % c, "lanes"], ["sc%d" % c], (), dve(512), name="scan" + nm)
            e0 = 512 * t + 128 * c
            if last:
                copy(T.ec[:, e0:e0 + 128], T.sc[:, j0 + 7:j0 + 1024:8], ["sc%d" % c], ["ec%d_%d" % (t, c)], 64, name="ec" + nm)
                send(home, guest, [([T.ec[:, e0:e0 + 128], T.ei[:, e0:e0 + 128]], T.ei[:, e0 + 512:e0 + 640])],
                     ["ec%d_%d" % (t, c), "ei%d" % t], ["ef%d" % c], name="s_e" + nm)
                dma("sp", [(T.ye[:, 128 * c:128 * c + 128], T.ei[:, e0 + 512:e0 + 640])], ["ef%d" % c], [], name="ye")
            elif c == NC - 1:
                copy(T.ec[:, 512 * t:512 * t + 512], T.sc[:, 7::8], ["sc%d" % k for k in range(NC)], ["ec%d_%d" % (t, k) for k in range(NC)], 256, name="ec" + nm)
                srcs = [T.ec[:, 512 * t:512 * t + 512]] + ([T.ei[:, 512 * t:512 * t + 512]] if t else [])
                send(nxt, prv, [(srcs, T.ei[:, 512 * t + 512:512 * t + 1024])],
                     ["ec%d_%d" % (t, k) for k in range(NC)] + (["ei%d" % t] if t else []), ["ei%d" % (t + 1)], lat=1000.0, name="s_e" + nm)
            if nm in SPLIT:
                for h in range(2):
                    gather(("act", "dve")[h], T.x2[:, j0 + 512 * h:j0 + 512 * h + 512], T.tab[:], T.ixl[:, 64 * c + 32 * h:64 * c + 32 * h + 32],
                           ["ixl%d" % c] + tabkeys, ["x2%d_%d" % (c, h)], 512, name="G2" + nm)
            else:
                gather("act", T.x2[:, j0:j0 + 1024], T.tab[:], T.ixl[:, 64 * c:64 * c + 64], ["ixl%d" % c] + tabkeys,
                       ["x2%d_%d" % (c, h) for h in range(2)], 1024, name="G2" + nm)
            bank = "px%d" % (c % 2)
            px = T[bank]
            mm([(px[:, k::8], T.x2[:, j0 + k:j0 + 1024:8], T.wq[:], k == 0, False) for k in range(8)]
               + [(px[:, 64 * u:64 * u + 64], T.idb[:], T.ot[:, s0:s0 + 64], False, u == 4) for u in range(5)],
               ["x2%d_%d" % (c, h) for h in range(2)] + [ko, "idb"] + wkeys, [bank], 832, name="ext" + nm)
            nb, pb, r0 = T.zn[:, 48 * c + 1:48 * c + 48:2, :], T.pb[:, 192 * c:192 * c + 192], 128 * c
            ts(nb, px[:, 0:192], 0.0, None, ALU.is_ge, None, [], ["zn%d" % c], 192, [bank], name="N" + nm)
            mm([(T.pl[:, 0:64], T.pick[:, 15 - i:143 - i], T.x2[:, j0 + i:j0 + 1024:16], i == 0, False) for i in range(16)],
               ["x2%d_%d" % (c, h) for h in range(2)] + ["pick"], ["pl"], 1024, name="backd" + nm)
            mm([x for u in range(3) for x in turn(T.pl[:, 0:64], T.zn, 3 * c + u, T.idb, False, u == 2)], ["zn%d" % c], ["pl"], 384, name="back" + nm)
            ts(T.rb[:, r0:r0 + 128], px[:, 192:320], 1.0, 0.0, ALU.add, ALU.max, [], ["rb%d" % c], 128, [bank], name="R" + nm)
            tt(pb, nb, px[:, 320:512], ALU.mult, ["zn%d" % c], ["pb%d" % c], 192, [bank], name="P" + nm)
            mm([(px[:, 0:64], T.idb[:], T.rb[:, r0:r0 + 64], True, False), (px[:, 0:64], T.idn[:], T.rb[:, r0 + 64:r0 + 128], False, False)]
               + [(px[:, 0:64], T.idn[:], T.pb[:, 192 * c + 64 * u:192 * c + 64 * u + 64], False, u == 2) for u in range(3)],
               ["pb%d" % c, "rb%d" % c, "idn"], [bank], 320, name="sum" + nm)
            if not last:
                ts(T.so[:, s0:s0 + 64], px[:, 0:64], -1.0, None, ALU.add, None, [], ["so" + nm], 64, [bank], name="oT" + nm)
                copy(T.sb[:, s0:s0 + 64], T.pl[:, 0:64], [], ["sb" + nm], 64, ["pl"], name="list1" + nm)
                send(nxt, prv, [([T.sb[:, s0:s0 + 64]], T.bl[:, s0 + 256:s0 + 320])], ["sb" + nm], ["bl%d_%d" % (t + 1, c)], name="s" + nm)
                if c % 2:
                    send(nxt, prv, [([T.so[:, s0 - 64:s0 + 64]], T.ot[:, s0 + 192:s0 + 320])], ["so%d%d" % (t, c - 1), "so" + nm],
                         ["ot%d_%d" % (t + 1, c - 1), "ot%d_%d" % (t + 1, c)], lat=200.0, name="s_o" + nm)
            else:
                tmp = T.tmp[:, 64 * c:64 * c + 64]
                ts(tmp, T.pl[:, 0:64], float(V), -float(V), ALU.is_ge, ALU.mult, [], ["tmp%d" % c], 64, ["pl"], name="mod" + nm)
                ts(T.zo[:, zpad, :], px[:, 0:64], -1.0, None, ALU.add, None, [], ["zo%d" % c], 64, [bank], name="oT" + nm)
                mm(turn(px[:, 64:128], T.zo, c, T.idb, True, True), ["zo%d" % c], [bank], 128, name="backo" + nm)
                tt(T.fs[:, 128 * c:128 * c + 64], tmp, T.pl[:, 0:64], ALU.add, ["tmp%d" % c], ["fb%d" % c], 64, ["pl"], name="fb" + nm)
                copy(T.fs[:, 128 * c + 64:128 * c + 128], px[:, 64:128], [], ["fo%d" % c], 64, [bank], name="fo" + nm)
                send(home, guest, [([T.fs[:, 128 * c:128 * c + 128]], T.fr[:, 128 * c:128 * c + 128])], ["fo%d" % c, "fb%d" % c], ["fr%d" % c], name="s" + nm)
                dma("sp", [(T.yb[:, 64 * c:64 * c + 64], T.fr[:, 128 * c:128 * c + 64])], ["fr%d" % c], [], name="yb")
                dma("act", [(T.yo[:, 64 * c:64 * c + 64], T.fr[:, 128 * c + 64:128 * c + 128])], ["fr%d" % c], [], name="yo")
    return ops


def link(ops):
    writer, readers, banker = {}, {}, {}
    for o in ops:
        deps = {}
        for k in o["r"]:
            if k in writer:
                deps[writer[k]] = True
        for k in o["w"]:
            if k in writer:
                deps[writer[k]] = True
            for x in readers.get(k, ()):
                deps[x] = True
        for k in o["banks"]:
            for x in banker.get(k, {}).values():
                deps.setdefault(x, False)
        deps.pop(o["i"], None)
        o["deps"] = deps
        for k in o["r"]:
            readers.setdefault(k, []).append(o["i"])
        for k in o["w"]:
            writer[k] = o["i"]
            readers[k] = []
        for k in o["banks"]:
            banker.setdefault(k, {})[o["eng"]] = o["i"]


def edges(ops, hop):
    out = []
    for o in ops:
        e, l = o["eng"], [(a["i"], 0.0) for a in o["after"]]
        for d, always in o["deps"].items():
            p = ops[d]
            l.append((d, 0.0 if e is None else hop if p["eng"] != e or p["kind"] == "dma" else 0.7 * hop if always and e != "pe" else 0.0))
        out.append(l)
    return out


def replay(order, ops, pre):
    free, end = {}, [0.0] * len(ops)
    for i in order:
        o = ops[i]
        s = free.get(o["eng"], 0.0)
        for d, gap in pre[i]:
            if end[d] + gap > s:
                s = end[d] + gap
        if o["eng"]:
            free[o["eng"]] = s + o["dur"]
        o["start"] = s
        end[i] = o["end"] = s + o["dur"] + o["lat"]
    return max(end)


def greedy(ops, pre, succ, pri, window):
    free, end = {}, [0.0] * len(ops)
    left = [len(l) for l in pre]
    ready = {i: 0.0 for i, l in enumerate(pre) if not l}
    order = []
    while ready:
        cands = [(max(s, free.get(ops[i]["eng"], 0.0)), i) for i, s in ready.items()]
        s0, i0 = min(cands)
        e = ops[i0]["eng"]
        s, i = max([x for x in cands if ops[x[1]]["eng"] == e and x[0] <= s0 + window], key=lambda x: (pri[x[1]], -x[1]))
        if e:
            free[e] = s + ops[i]["dur"]
        end[i] = s + ops[i]["dur"] + ops[i]["lat"]
        order.append(i)
        del ready[i]
        for x in succ[i]:
            left[x] -= 1
            if left[x] == 0:
                ready[x] = max(end[d] + gap for d, gap in pre[x])
    return order


PLAN = []


def arrange(T, topo, core):
    if PLAN:
        return PLAN[0]
    sets = []
    for P in GUESS:
        ops = build(T, topo, core, P)
        link(ops)
        sets.append((ops, edges(ops, P["hop"])))
    ops, pre = sets[0]
    succ = [[] for _ in ops]
    for i, l in enumerate(pre):
        for d, _ in l:
            succ[d].append(i)
    pri = [0.0] * len(ops)
    for i in range(len(ops) - 1, -1, -1):
        pri[i] = ops[i]["dur"] + ops[i]["lat"] + max([GUESS[0]["hop"] + pri[s] for s in succ[i]] + [0.0])
    for i, o in enumerate(ops):
        if o["name"][-2:].isdigit():
            pri[i] = -1000.0 * (NC * int(o["name"][-2]) + int(o["name"][-1]) + LATER.get(o["name"][:-2], 0.0)) + 1e-3 * pri[i]
        pri[i] += o.get("bonus", 0.0)
    seed = [SEED]

    def rnd():
        seed[0] = (seed[0] * 1103515245 + 12345) % 2147483648
        return seed[0] / 2147483648.0

    eng = [o["eng"] for o in ops]
    fixed = ["bonus" in o for o in ops]
    flat = [([o["dur"] for o in s], [o["dur"] + o["lat"] for o in s], p) for s, p in sets]

    def run(order):
        total, pairs = 0.0, []
        for dur, span, prev in flat:
            free, lastop, end, why = {}, {}, [0.0] * len(ops), [-1] * len(ops)
            for i in order:
                e = eng[i]
                s, w = free.get(e, 0.0), -2 - lastop.get(e, -1)
                for d, gap in prev[i]:
                    if end[d] + gap >= s:
                        s, w = end[d] + gap, d
                if e:
                    free[e], lastop[e] = s + dur[i], i
                end[i], why[i] = s + span[i], w
            top = max(end)
            total += top
            i = end.index(top)
            while why[i] != -1:
                if why[i] < -1:
                    pairs.append((-2 - why[i], i))
                    i = -2 - why[i]
                else:
                    i = why[i]
        return total / len(flat), pairs

    def swap(order, j, i):
        a, b = order.index(j), order.index(i)
        need = set(d for d, _ in pre[i])
        front, back = [i], []
        for x in order[b - 1:a - 1 if a else None:-1]:
            if x in need:
                front.append(x)
                need.update(d for d, _ in pre[x])
            else:
                back.append(x)
        if j in need or fixed[j]:
            return None
        return order[:a] + front[::-1] + back[::-1] + order[b + 1:]

    def by_key(key):
        left = [len(l) for l in pre]
        ready, out = [i for i, l in enumerate(pre) if not l], []
        while ready:
            i = min(ready, key=key.get)
            ready.remove(i)
            out.append(i)
            for x in succ[i]:
                left[x] -= 1
                if left[x] == 0:
                    ready.append(x)
        return out

    order = greedy(ops, pre, succ, pri, WINDOW)
    replay(order, ops, pre)
    begin = min(o["start"] for o in ops if o["name"][:2] == "G2")
    seen, slot = {}, {}
    for o in ops:
        if o["name"][-2:].isdigit() and (o["name"][-2] != "0" or o["start"] >= begin):
            seen[o["name"]] = seen.get(o["name"], 0) + 1
            slot[o["i"]] = (o["name"][:-2] + "ab"[seen[o["name"]] - 1], NC * int(o["name"][-2]) + int(o["name"][-1]))
    place = dict(PLACE)

    def keyed(pl):
        return by_key({o["i"]: begin + 3000.0 * (slot[o["i"]][1] + pl.get(slot[o["i"]][0], 1.0)) if o["i"] in slot
                       else o["start"] if o["eng"] else -1.0 for o in ops})

    kinds = sorted(place)
    order = keyed(place)
    now, pairs = run(order)
    for k in range(ROUNDS0):
        new = dict(place)
        for _ in range(1 + int(2 * rnd())):
            new[kinds[int(rnd() * len(kinds))]] += (rnd() - 0.5) * rnd() * 1.5
        cand = keyed(new)
        c, p = run(cand)
        if c <= now + 0.3 * HEAT * -math.log(rnd() + 1e-9):
            now, pairs, order, place = c, p, cand, new
    FOUND.append(place)
    best, top = now, order
    for k in range(ROUNDS):
        if rnd() < 0.8 and pairs:
            j, i = pairs[int(rnd() * len(pairs))]
        else:
            b = 1 + int(rnd() * (len(order) - 1))
            i = order[b]
            same = [x for x in order[max(0, b - 30):b] if eng[x] == eng[i]]
            if not same or not eng[i]:
                continue
            j = same[-1 - int(rnd() * min(3, len(same)))]
        cand = swap(order, j, i)
        if cand is None:
            continue
        c, p = run(cand)
        if c <= now + HEAT * (1.0 - k / ROUNDS) * -math.log(rnd() + 1e-9):
            now, pairs, order = c, p, cand
            if c < best:
                best, top = c, cand
    PLAN.append(top)
    return top


def rank_program(g, core, T, topo):
    if T.rank_of(core) is None:
        return
    ops = build(T, topo, core, GUESS[0])
    link(ops)
    order = arrange(T, topo, core)
    replay(order, ops, edges(ops, GUESS[0]["hop"]))
    for o in ops:
        o["on"] = o["eng"]
    order = [ops[i] for i in order]
    queue = {"pe": g.tensor, "dve": g.vector, "act": g.scalar, "pool": g, "sp": g.sync}
    known = {e: {} for e in queue}
    done = {e: 0 for e in queue}
    total = {"sent": 0}
    for o in order:
        e = o["on"]
        if e is None:
            o["seen"] = {o["tok"][0]: o["tok"][1]}
            total[o["tok"][0]] = o["tok"][1]
            continue
        q, kn = queue[e], known[e]
        need = {}
        for d, always in o["deps"].items():
            p = ops[d]
            if p["kind"] == "rem" or (p["on"] == e and p["kind"] != "dma" and (e == "pe" or not always)):
                continue
            need[d] = p
        for p in sorted(need.values(), key=lambda x: -x["end"]):
            sem, val = p["tok"]
            if kn.get(sem, 0) < val:
                q.wait_ge(T.sem[sem], val)
                for k, v in p["seen"].items():
                    kn[k] = max(kn.get(k, 0), v)
        if o["kind"] == "rem":
            o["fn"](q)
            total["sent"] += o["sent"]
            continue
        if o["kind"] == "dma":
            o["fn"](q)
        else:
            ins = o["fn"](q, e) if o["kind"] == "g" else o["fn"](q)
            done[e] += 1
            o["tok"] = ("e_" + e, done[e])
            ins.then_inc(T.sem["e_" + e], 1)
        o["seen"] = dict(kn)
        o["seen"][o["tok"][0]] = o["tok"][1]
        total[o["tok"][0]] = o["tok"][1]
    for sem, val in total.items():
        if val:
            g.wait_ge(T.sem[sem], val)
